import numpy as np
import ml_dtypes


def mxq(x, axis, fmt="e4m3"):
    dtype, down = {"e4m3": (ml_dtypes.float8_e4m3fn, 7), "e5m2": (ml_dtypes.float8_e5m2, 14)}[fmt]
    v = np.moveaxis(np.asarray(x, np.float32).astype(ml_dtypes.bfloat16).astype(np.float64), axis, -1)
    blocks = v.reshape(v.shape[:-1] + (-1, 32))
    amax = np.abs(blocks).max(-1, keepdims=True)
    byte = np.maximum(np.where(amax > 0, np.frexp(amax)[1] - 1 + 127, 0) - down, 1)
    scale = np.exp2(byte - 127.0)
    codes = (blocks / scale).astype(np.float32).astype(dtype).astype(np.float64)
    return np.moveaxis((codes * scale).reshape(v.shape), -1, axis)


WIDE = False


def mx_kscale(k):
    if not WIDE:
        return np.ones(k)
    levels = np.array([30, -30])
    if k % 512:
        return np.exp2(np.random.permutation(np.resize(levels, k // 32))).repeat(32)
    a = np.empty((k // 512, 16))
    for p in range(k // 512):
        a[p, :8] = np.random.permutation(np.resize(levels, 8))
        for g in range(8):
            far = levels[np.abs(levels - a[p, g]) >= 10]
            a[p, g + 8] = far[np.random.randint(len(far))]
    return np.exp2(a.ravel()).repeat(32)


def f64(x):
    return np.asarray(x).astype(np.float64)


def striped(idx):
    return np.tile(np.asarray(idx).reshape(-1, 16).T, (8, 1)).astype(np.uint16)


def unstriped(offs):
    return offs[:16].T.reshape(-1).astype(np.int64)


E2M1 = np.array([0.0, 0.5, 1.0, 1.5, 2.0, 3.0, 4.0, 6.0, -0.0, -0.5, -1.0, -1.5, -2.0, -3.0, -4.0, -6.0])


def pack_weight(w, fmt):
    k, n = w.shape
    w = f64(np.asarray(w, np.float32).astype(ml_dtypes.bfloat16)).reshape(k // 32, 32, n)
    amax = np.abs(w).max(1)
    if fmt in ("e4m3", "e5m2"):
        byte = np.frexp(amax)[1] - 1 + 127 - (7 if fmt == "e4m3" else 14)
    else:
        mant, ex = np.frexp(amax / 6.0)
        byte = np.where(mant > 0.5, ex, ex - 1) + 127
    byte = np.clip(np.where(amax > 0, byte, 1), 1, 254)
    scaled = (w * np.exp2(127.0 - byte)[:, None, :]).reshape(k, n).astype(np.float32)
    by_word = np.ascontiguousarray(scaled.reshape(k // 512, 128, 4, n).transpose(0, 1, 3, 2))
    if fmt in ("e4m3", "e5m2"):
        words = by_word.astype(ml_dtypes.float8_e4m3fn if fmt == "e4m3" else ml_dtypes.float8_e5m2).view(np.uint8)
    else:
        c = by_word.astype(ml_dtypes.float4_e2m1fn).view(np.uint8) & 0xF
        words = (c[..., 0::2] | (c[..., 1::2] << 4)).reshape(k // 512, 128, 2 * n)
    return np.ascontiguousarray(words), np.ascontiguousarray(byte.astype(np.uint8).reshape(k // 512, 16, n))


def unpack_weight(words, scales, fmt):
    g, _, n = scales.shape
    words = np.ascontiguousarray(words).reshape(g, 128, n, -1)
    if fmt in ("e4m3", "e5m2"):
        vals = words.view(ml_dtypes.float8_e4m3fn if fmt == "e4m3" else ml_dtypes.float8_e5m2).astype(np.float64)
    else:
        nib = np.empty((g, 128, n, 4), np.uint8)
        nib[..., 0::2] = words & 0xF
        nib[..., 1::2] = words >> 4
        vals = E2M1[nib]
    vals = vals * np.repeat(np.exp2(scales.astype(np.float64) - 127.0), 8, axis=1)[..., None]
    return vals.transpose(0, 1, 3, 2).reshape(g * 512, n)


K, T, J, R, F, Z, I, O, N, S = 512, 1024, 256, 512, 512, 1024, 256, 128, 256, 1024


def setup_inputs():
    n = np.random.standard_normal
    idx = np.random.permutation(T)[:J]
    idx2 = np.random.permutation(Z)[:J]
    idx3 = np.random.permutation(J)[:I]
    idx4 = np.random.permutation(J)[:I]
    idx5 = np.random.permutation(I)[:O]
    idx6 = np.random.permutation(I)[:O]
    idx7 = np.random.permutation(S)[:N]
    fk = mx_kscale(K)
    ff = mx_kscale(F)
    fr = mx_kscale(R)
    xtp = pack_weight(n((K, T)) / fk[:, None], "e2m1")
    xop = pack_weight(n((F, Z)) / ff[:, None], "e5m2")
    wp = pack_weight(n((K, R)) * 1 / np.sqrt(K) * fk[:, None] * fr, "e5m2")
    w2p = pack_weight(n((F, R)) * 1 / np.sqrt(F) * ff[:, None], "e4m3")
    vsp = pack_weight(n((R, S)) * 1 / np.sqrt(R) / fr[:, None], "e4m3")
    return {
        "xt_words": xtp[0],
        "xt_scales": xtp[1],
        "xo_words": xop[0],
        "xo_scales": xop[1],
        "w_words": wp[0],
        "w_scales": wp[1],
        "w2_words": w2p[0],
        "w2_scales": w2p[1],
        "vs_words": vsp[0],
        "vs_scales": vsp[1],
        "offs": striped(idx),
        "offs2": striped(idx2),
        "offs3": striped(idx3),
        "offs4": striped(idx4),
        "offs5": striped(idx5),
        "offs6": striped(idx6),
        "offs7": striped(idx7),
    }


def reference(xt_words, xt_scales, xo_words, xo_scales, w_words, w_scales, w2_words, w2_scales, vs_words, vs_scales, offs, offs2, offs3, offs4, offs5, offs6, offs7):
    idx = unstriped(offs)
    idx2 = unstriped(offs2)
    idx3 = unstriped(offs3)
    idx4 = unstriped(offs4)
    idx5 = unstriped(offs5)
    idx6 = unstriped(offs6)
    idx7 = unstriped(offs7)
    xtu = unpack_weight(xt_words, xt_scales, "e2m1")
    xou = unpack_weight(xo_words, xo_scales, "e5m2")
    wu = unpack_weight(w_words, w_scales, "e5m2")
    w2u = unpack_weight(w2_words, w2_scales, "e4m3")
    vsu = unpack_weight(vs_words, vs_scales, "e4m3")
    xtidxg = xtu[:, idx]
    a = wu.T @ xtidxg
    xoidx2g = xou[:, idx2]
    b = w2u.T @ xoidx2g
    lb = b[:, 0:1]
    la = a[:, 0:1]
    h1 = np.maximum(a[:, idx3] * lb, b[:, idx4] * la)
    hid = np.abs(h1[:, idx5] - h1[:, idx6])
    vsidx7g = vsu[:, idx7]
    hidq = mxq(hid, 0, "e5m2")
    y = vsidx7g.T @ hidq
    return y

@@ -1,0 +1,186 @@
+from contextlib import ExitStack
+
+import concourse.mybir as mybir
+
+F32 = mybir.dt.float32
+BF16 = mybir.dt.bfloat16
+I32 = mybir.dt.int32
+U32 = mybir.dt.uint32
+U16 = mybir.dt.uint16
+U8 = mybir.dt.uint8
+E2M1X4 = mybir.dt.float4_e2m1fn_x4
+E5M2X4 = mybir.dt.float8_e5m2_x4
+E4M3X4 = mybir.dt.float8_e4m3fn_x4
+ALU = mybir.AluOpType
+ACT = mybir.ActivationFunctionType
+
+P = 128
+PACK = 4
+T, J, R, I, O, N = 1024, 256, 512, 256, 128, 256
+WIDE = 2 * J
+FLOPS = 2 * 512 * R * J * 2 + 2 * R * N * O
+
+
+def tile_list_leadmeetthenlook_twotab_store_plain_kernel(
+    tc, xt_words, xt_scales, xo_words, xo_scales, w_words, w_scales, w2_words, w2_scales, vs_words, vs_scales,
+    offs, offs2, offs3, offs4, offs5, offs6, offs7, out,
+):
+    nc = tc.nc
+    with ExitStack() as ctx:
+        sb = ctx.enter_context(tc.tile_pool(name="sb", bufs=1))
+        ps = ctx.enter_context(tc.psum_pool(name="ps", bufs=1))
+
+        def load_list(src, name):
+            tile = sb.tile(list(src.shape), U16, name=name)
+            nc.sync.dma_start(tile[:], src)
+            return tile
+
+        def load_words(queue, src, name):
+            tile = sb.tile([P, src.shape[2]], U32, name=name, align_bytes=64)
+            queue.dma_start(tile[:].bitcast(I32), src[0].rearrange("p c t -> p (c t)").bitcast(I32))
+            return tile
+
+        def zero_plane(engine, width, name):
+            tile = sb.tile([P, width], U8, name=name, align_bytes=64)
+            engine.memset(tile[:].bitcast(I32), 0)
+            return tile
+
+        def load_plane(queue, tile, src, rows=range(PACK)):
+            for r in rows:
+                queue.dma_start(tile[r:P:32, :].bitcast(I32), src[0, r:16:PACK, :].bitcast(I32))
+
+        def zero_stage(engine, base, width, name):
+            tile = sb.tile([P, 2, width], U8, name=name, align_bytes=64)
+            engine.memset(tile[base : base + 64].rearrange("p h c -> p (h c)").bitcast(I32), 0)
+            return tile
+
+        def load_stage(queue, tile, base, src):
+            rows = src[0].bitcast(I32).rearrange("(h q r) c -> q r h c", h=2, q=2)
+            for q in range(2):
+                queue.dma_start(tile[base + 32 * q : base + 32 * q + PACK].bitcast(I32), rows[q])
+
+        def move_half(plane, h, stage, base):
+            nc.vector.tensor_copy(plane[64 * h : 64 * h + 64].bitcast(I32), stage[base : base + 64, h, :].bitcast(I32))
+
+        def gather(window, offsets, name):
+            tile = sb.tile([P, 16 * offsets.shape[1]], window.dtype, name=name, align_bytes=64)
+            nc.vector.tensor_copy(tile[:], window[:].indirect(offsets[:]))
+            return tile
+
+        def load_xt():
+            tile = sb.tile([P, T], U16, name="xt_w", align_bytes=64)
+            nc.sync.dma_start(tile[:].bitcast(I32), xt_words[0].bitcast(I32))
+            return tile
+
+        def deal(engine_copy, src, name):
+            tile = sb.tile([P, R], src.dtype, name=name, align_bytes=64)
+            engine_copy(tile[:].rearrange("p (t c i) -> p c t i", t=PACK, i=4), src[:].rearrange("p (c i t) -> p c t i", t=PACK, i=4))
+            return tile
+
+        def deal_bytes(src, name):
+            tile = sb.tile([P, R], U8, name=name, align_bytes=64)
+            nc.vector.tensor_copy(tile[:].rearrange("p (t m) -> p t m", t=PACK), src.rearrange("p (m t) -> p t m", t=PACK))
+            return tile
+
+        xt_st = zero_stage(nc.vector, 0, T, "xt_st")
+        w_st = zero_stage(nc.gpsimd, 0, R, "w_st")
+        xo_st = zero_stage(nc.vector, 64, T, "xo_st")
+        w2_st = zero_stage(nc.gpsimd, 64, R, "w2_st")
+        vs_s = zero_plane(nc.gpsimd, T, "vs_s")
+        l1 = load_list(offs, "l1")
+        xt_w = load_xt()
+        load_stage(nc.sync, xt_st, 0, xt_scales)
+        load_stage(nc.sync, w_st, 0, w_scales)
+        w_w = load_words(nc.sync, w_words, "w_w")
+        xo_w = load_words(nc.sync, xo_words, "xo_w")
+        l2 = load_list(offs2, "l2")
+        w2_w = load_words(nc.sync, w2_words, "w2_w")
+        load_stage(nc.sync, xo_st, 64, xo_scales)
+        load_stage(nc.sync, w2_st, 64, w2_scales)
+        l4 = load_list(offs4, "l4")
+        l3 = load_list(offs3, "l3")
+        vs_w = load_words(nc.sync, vs_words, "vs_w")
+        l7 = load_list(offs7, "l7")
+        load_plane(nc.sync, vs_s, vs_scales)
+        l6 = load_list(offs6, "l6")
+        l5 = load_list(offs5, "l5")
+
+        xt_s = sb.tile([P, T], U8, name="xt_s", align_bytes=64)
+        xo_s = sb.tile([P, T], U8, name="xo_s", align_bytes=64)
+        move_half(xt_s, 0, xt_st, 0)
+        move_half(xt_s, 1, xt_st, 0)
+        move_half(w_st[:, 0, :], 1, w_st, 0)
+        xt_g = gather(xt_w, l1, "xt_g")
+        xts_g = gather(xt_s, l1, "xts_g")
+        ws_d = deal_bytes(w_st[:, 0, :], "ws_d")
+        w_d = deal(nc.scalar.copy, w_w, "w_d")
+        w2_d = deal(nc.scalar.copy, w2_w, "w2_d")
+        xo_g = gather(xo_w, l2, "xo_g")
+        move_half(xo_s, 0, xo_st, 64)
+        move_half(w2_st[:, 1, :], 0, w2_st, 64)
+        move_half(xo_s, 1, xo_st, 64)
+        w2s_d = deal_bytes(w2_st[:, 1, :], "w2s_d")
+        xos_g = gather(xo_s, l2, "xos_g")
+
+        a_sb, b_sb = [], []
+        for t in range(PACK):
+            cols = slice(t * P, (t + 1) * P)
+            acc = ps.tile([P, J], F32, name="acc_a%d" % t, tag="bank%d" % t)
+            nc.tensor.matmul_mx(out=acc[:], lhsT=w_d[:, cols].bitcast(E5M2X4), lhsT_scale=ws_d[:, cols],
+                                rhs=xt_g[:].bitcast(E2M1X4), rhs_scale=xts_g[:], start=True, stop=True)
+            rows = sb.tile([P, WIDE], F32, name="a%d" % t)
+            nc.scalar.copy(rows[:, :J], acc[:])
+            a_sb.append(rows)
+
+        for t in range(PACK):
+            cols = slice(t * P, (t + 1) * P)
+            acc = ps.tile([P, J], F32, name="acc_b%d" % t, tag="bank%d" % (PACK + t))
+            nc.tensor.matmul_mx(out=acc[:], lhsT=w2_d[:, cols].bitcast(E4M3X4), lhsT_scale=w2s_d[:, cols],
+                                rhs=xo_g[:].bitcast(E5M2X4), rhs_scale=xos_g[:], start=True, stop=True)
+            rows = sb.tile([P, WIDE], F32, name="b%d" % t)
+            nc.vector.tensor_copy(rows[:, :J], acc[:])
+            b_sb.append(rows)
+
+        vs_g = gather(vs_w, l7, "vs_g")
+        vss_g = gather(vs_s, l7, "vss_g")
+
+        diff = sb.tile([P, PACK, O], F32, name="diff")
+
+        def place(t):
+            second = sb.tile([P, O], F32, name="second%d" % t)
+            if t < 2:
+                nc.scalar.activation(second[:], h1[t][:].indirect(l6[:]), ACT.Copy)
+            else:
+                nc.vector.tensor_copy(second[:], h1[t][:].indirect(l6[:]))
+            nc.vector.tensor_tensor(diff[:, t, :], h1[t][:].indirect(l5[:]), second[:], ALU.subtract)
+
+        h1 = []
+        for t in range(PACK):
+            pa = sb.tile([P, I], F32, name="pa%d" % t)
+            pb = sb.tile([P, I], F32, name="pb%d" % t)
+            nc.scalar.activation(pb[:], b_sb[t][:].indirect(l4[:]), ACT.Copy, scale=a_sb[t][:, 0:1])
+            nc.scalar.activation(pa[:], a_sb[t][:].indirect(l3[:]), ACT.Copy, scale=b_sb[t][:, 0:1])
+            kept = sb.tile([P, I], F32, name="h1_%d" % t)
+            nc.vector.tensor_tensor(kept[:], pa[:], pb[:], ALU.max)
+            h1.append(kept)
+            if t > 0:
+                place(t - 1)
+        place(PACK - 1)
+
+        hid = sb.tile([P, O, PACK], BF16, name="hid", align_bytes=64)
+        woven = diff[:].rearrange("p t o -> p o t")
+        half = O // 2
+        nc.scalar.activation(hid[:, :half, :], woven[:, :half, :], ACT.Abs)
+        nc.vector.scalar_tensor_tensor(hid[:, half:, :], woven[:, half:, :], -1.0, woven[:, half:, :], ALU.mult, ALU.max)
+        hid_w = sb.tile([P, O], U32, name="hid_w", align_bytes=64)
+        hid_s = sb.tile([P, O], U8, name="hid_s", align_bytes=64)
+        nc.vector.quantize_mx(out=hid_w[:].bitcast(E5M2X4), scales=hid_s[:], in_=hid[:].rearrange("p o t -> p (o t)"))
+
+        for h, (copy, queue) in enumerate(((nc.vector.tensor_copy, nc.sync), (nc.scalar.copy, nc.scalar))):
+            cols = slice(h * P, (h + 1) * P)
+            acc = ps.tile([P, O], F32, name="acc_y%d" % h, tag="bank%d" % h)
+            nc.tensor.matmul_mx(out=acc[:], lhsT=vs_g[:, cols].bitcast(E4M3X4), lhsT_scale=vss_g[:, cols],
+                                rhs=hid_w[:].bitcast(E5M2X4), rhs_scale=hid_s[:], start=True, stop=True)
+            y = sb.tile([P, O], F32, name="y%d" % h)
+            copy(y[:], acc[:])
+            queue.dma_start(out[cols, :], y[:])

@@ -97,13 +97,13 @@ def tile_list_leadmeetthenlook_twotab_store_plain_kernel(
         w2_w = load_words(nc.sync, w2_words, "w2_w")
         load_stage(nc.sync, xo_st, 64, xo_scales)
         load_stage(nc.sync, w2_st, 64, w2_scales)
-        l4 = load_list(offs4, "l4")
-        l3 = load_list(offs3, "l3")
         vs_w = load_words(nc.sync, vs_words, "vs_w")
         l7 = load_list(offs7, "l7")
-        load_plane(nc.sync, vs_s, vs_scales)
+        l4 = load_list(offs4, "l4")
+        l3 = load_list(offs3, "l3")
         l6 = load_list(offs6, "l6")
         l5 = load_list(offs5, "l5")
+        load_plane(nc.sync, vs_s, vs_scales)
 
         xt_s = sb.tile([P, T], U8, name="xt_s", align_bytes=64)
         xo_s = sb.tile([P, T], U8, name="xo_s", align_bytes=64)
@@ -146,35 +146,36 @@ def tile_list_leadmeetthenlook_twotab_store_plain_kernel(
 
         diff = sb.tile([P, PACK, O], F32, name="diff")
 
-        def place(t):
+        def place(t, parts):
             second = sb.tile([P, O], F32, name="second%d" % t)
-            if t < 2:
-                nc.scalar.activation(second[:], h1[t][:].indirect(l6[:]), ACT.Copy)
-            else:
-                nc.vector.tensor_copy(second[:], h1[t][:].indirect(l6[:]))
-            nc.vector.tensor_tensor(diff[:, t, :], h1[t][:].indirect(l5[:]), second[:], ALU.subtract)
+            for cols, entries in parts:
+                if t >= 2:
+                    nc.scalar.activation(second[:, cols], h1[t][:].indirect(l6[:, entries]), ACT.Copy)
+                else:
+                    nc.vector.tensor_copy(second[:, cols], h1[t][:].indirect(l6[:, entries]))
+            for cols, entries in parts:
+                nc.vector.tensor_tensor(diff[:, t, cols], h1[t][:].indirect(l5[:, entries]), second[:, cols], ALU.subtract)
 
+        whole = [(slice(0, O), slice(0, O // 16))]
+        halves = [(slice(0, O // 2), slice(0, O // 32)), (slice(O // 2, O), slice(O // 32, O // 16))]
         h1 = []
         for t in range(PACK):
-            pa = sb.tile([P, I], F32, name="pa%d" % t)
-            pb = sb.tile([P, I], F32, name="pb%d" % t)
+            pa = sb.tile([P, I], F32, name="pa%d" % t, tag="pa", bufs=2)
+            pb = sb.tile([P, I], F32, name="pb%d" % t, tag="pb", bufs=2)
             nc.scalar.activation(pb[:], b_sb[t][:].indirect(l4[:]), ACT.Copy, scale=a_sb[t][:, 0:1])
             nc.scalar.activation(pa[:], a_sb[t][:].indirect(l3[:]), ACT.Copy, scale=b_sb[t][:, 0:1])
             kept = sb.tile([P, I], F32, name="h1_%d" % t)
             nc.vector.tensor_tensor(kept[:], pa[:], pb[:], ALU.max)
             h1.append(kept)
-            if t > 0:
-                place(t - 1)
-        place(PACK - 1)
+            place(t, whole if t < PACK - 1 else halves)
 
         hid = sb.tile([P, O, PACK], BF16, name="hid", align_bytes=64)
         woven = diff[:].rearrange("p t o -> p o t")
-        half = O // 2
-        nc.scalar.activation(hid[:, :half, :], woven[:, :half, :], ACT.Abs)
-        nc.vector.scalar_tensor_tensor(hid[:, half:, :], woven[:, half:, :], -1.0, woven[:, half:, :], ALU.mult, ALU.max)
         hid_w = sb.tile([P, O], U32, name="hid_w", align_bytes=64)
         hid_s = sb.tile([P, O], U8, name="hid_s", align_bytes=64)
-        nc.vector.quantize_mx(out=hid_w[:].bitcast(E5M2X4), scales=hid_s[:], in_=hid[:].rearrange("p o t -> p (o t)"))
+        for cols, entries in halves:
+            nc.scalar.activation(hid[:, cols, :], woven[:, cols, :], ACT.Abs)
+            nc.vector.quantize_mx(out=hid_w[:, cols].bitcast(E5M2X4), scales=hid_s[:, cols], in_=hid[:, cols, :].rearrange("p o t -> p (o t)"))
 
         for h, (copy, queue) in enumerate(((nc.vector.tensor_copy, nc.sync), (nc.scalar.copy, nc.scalar))):
             cols = slice(h * P, (h + 1) * P)

@@ -84,9 +84,10 @@ def tile_list_leadmeetthenlook_twotab_store_plain_kernel(
 
         xt_st = zero_stage(nc.vector, 0, T, "xt_st")
         w_st = zero_stage(nc.gpsimd, 0, R, "w_st")
-        xo_st = zero_stage(nc.vector, 64, T, "xo_st")
         w2_st = zero_stage(nc.gpsimd, 64, R, "w2_st")
+        xo_s = zero_plane(nc.vector, T, "xo_s")
         vs_s = zero_plane(nc.gpsimd, T, "vs_s")
+        load_plane(nc.gpsimd, vs_s, vs_scales)
         l1 = load_list(offs, "l1")
         xt_w = load_xt()
         load_stage(nc.sync, xt_st, 0, xt_scales)
@@ -95,18 +96,16 @@ def tile_list_leadmeetthenlook_twotab_store_plain_kernel(
         xo_w = load_words(nc.sync, xo_words, "xo_w")
         l2 = load_list(offs2, "l2")
         w2_w = load_words(nc.sync, w2_words, "w2_w")
-        load_stage(nc.sync, xo_st, 64, xo_scales)
+        load_plane(nc.sync, xo_s, xo_scales)
         load_stage(nc.sync, w2_st, 64, w2_scales)
-        vs_w = load_words(nc.sync, vs_words, "vs_w")
-        l7 = load_list(offs7, "l7")
         l4 = load_list(offs4, "l4")
         l3 = load_list(offs3, "l3")
+        vs_w = load_words(nc.sync, vs_words, "vs_w")
+        l7 = load_list(offs7, "l7")
         l6 = load_list(offs6, "l6")
         l5 = load_list(offs5, "l5")
-        load_plane(nc.sync, vs_s, vs_scales)
 
         xt_s = sb.tile([P, T], U8, name="xt_s", align_bytes=64)
-        xo_s = sb.tile([P, T], U8, name="xo_s", align_bytes=64)
         move_half(xt_s, 0, xt_st, 0)
         move_half(xt_s, 1, xt_st, 0)
         move_half(w_st[:, 0, :], 1, w_st, 0)
@@ -116,9 +115,7 @@ def tile_list_leadmeetthenlook_twotab_store_plain_kernel(
         w_d = deal(nc.scalar.copy, w_w, "w_d")
         w2_d = deal(nc.scalar.copy, w2_w, "w2_d")
         xo_g = gather(xo_w, l2, "xo_g")
-        move_half(xo_s, 0, xo_st, 64)
         move_half(w2_st[:, 1, :], 0, w2_st, 64)
-        move_half(xo_s, 1, xo_st, 64)
         w2s_d = deal_bytes(w2_st[:, 1, :], "w2s_d")
         xos_g = gather(xo_s, l2, "xos_g")
 

@@ -16,7 +16,11 @@ ACT = mybir.ActivationFunctionType
 
 P = 128
 PACK = 4
-T, J, R, I, O, N = 1024, 256, 512, 256, 128, 256
+QUADRANT = 32
+HALF = 64
+PER_COLUMN = 16
+TABLE = 1024
+J, R, I, O, N = 256, 512, 256, 128, 256
 WIDE = 2 * J
 FLOPS = 2 * 512 * R * J * 2 + 2 * R * N * O
 
@@ -35,150 +39,174 @@ def tile_list_leadmeetthenlook_twotab_store_plain_kernel(
             nc.sync.dma_start(tile[:], src)
             return tile
 
-        def load_words(queue, src, name):
+        def load_words(src, name):
             tile = sb.tile([P, src.shape[2]], U32, name=name, align_bytes=64)
-            queue.dma_start(tile[:].bitcast(I32), src[0].rearrange("p c t -> p (c t)").bitcast(I32))
+            nc.sync.dma_start(tile[:].bitcast(I32), src[0].rearrange("p c t -> p (c t)").bitcast(I32))
             return tile
 
-        def zero_plane(engine, width, name):
-            tile = sb.tile([P, width], U8, name=name, align_bytes=64)
+        def zero_plane(engine, name):
+            tile = sb.tile([P, TABLE], U8, name=name, align_bytes=64)
             engine.memset(tile[:].bitcast(I32), 0)
             return tile
 
-        def load_plane(queue, tile, src, rows=range(PACK)):
-            for r in rows:
-                queue.dma_start(tile[r:P:32, :].bitcast(I32), src[0, r:16:PACK, :].bitcast(I32))
+        def load_plane(queue, plane, src):
+            for r in range(PACK):
+                queue.dma_start(plane[r:P:QUADRANT, :].bitcast(I32), src[0, r:16:PACK, :].bitcast(I32))
 
         def zero_stage(engine, base, width, name):
             tile = sb.tile([P, 2, width], U8, name=name, align_bytes=64)
-            engine.memset(tile[base : base + 64].rearrange("p h c -> p (h c)").bitcast(I32), 0)
+            engine.memset(tile[base : base + HALF].rearrange("p h c -> p (h c)").bitcast(I32), 0)
             return tile
 
-        def load_stage(queue, tile, base, src):
+        def load_stage(stage, base, src):
             rows = src[0].bitcast(I32).rearrange("(h q r) c -> q r h c", h=2, q=2)
             for q in range(2):
-                queue.dma_start(tile[base + 32 * q : base + 32 * q + PACK].bitcast(I32), rows[q])
+                first = base + QUADRANT * q
+                nc.sync.dma_start(stage[first : first + PACK].bitcast(I32), rows[q])
 
         def move_half(plane, h, stage, base):
-            nc.vector.tensor_copy(plane[64 * h : 64 * h + 64].bitcast(I32), stage[base : base + 64, h, :].bitcast(I32))
+            nc.vector.tensor_copy(
+                plane[HALF * h : HALF * (h + 1)].bitcast(I32), stage[base : base + HALF, h, :].bitcast(I32)
+            )
+
+        def entries(offsets, picks):
+            return offsets[:, picks.start // PER_COLUMN : picks.stop // PER_COLUMN]
 
         def gather(window, offsets, name):
-            tile = sb.tile([P, 16 * offsets.shape[1]], window.dtype, name=name, align_bytes=64)
+            tile = sb.tile([P, PER_COLUMN * offsets.shape[1]], window.dtype, name=name, align_bytes=64)
             nc.vector.tensor_copy(tile[:], window[:].indirect(offsets[:]))
             return tile
 
-        def load_xt():
-            tile = sb.tile([P, T], U16, name="xt_w", align_bytes=64)
-            nc.sync.dma_start(tile[:].bitcast(I32), xt_words[0].bitcast(I32))
+        def deal_words(src, name):
+            tile = sb.tile([P, R], U32, name=name, align_bytes=64)
+            nc.scalar.copy(
+                tile[:].rearrange("p (t c i) -> p c t i", t=PACK, i=4),
+                src[:].rearrange("p (c i t) -> p c t i", t=PACK, i=4),
+            )
             return tile
 
-        def deal(engine_copy, src, name):
-            tile = sb.tile([P, R], src.dtype, name=name, align_bytes=64)
-            engine_copy(tile[:].rearrange("p (t c i) -> p c t i", t=PACK, i=4), src[:].rearrange("p (c i t) -> p c t i", t=PACK, i=4))
-            return tile
-
-        def deal_bytes(src, name):
+        def deal_bytes(plane, name):
             tile = sb.tile([P, R], U8, name=name, align_bytes=64)
-            nc.vector.tensor_copy(tile[:].rearrange("p (t m) -> p t m", t=PACK), src.rearrange("p (m t) -> p t m", t=PACK))
+            nc.vector.tensor_copy(
+                tile[:].rearrange("p (t m) -> p t m", t=PACK), plane.rearrange("p (m t) -> p t m", t=PACK)
+            )
             return tile
 
-        xt_st = zero_stage(nc.vector, 0, T, "xt_st")
-        w_st = zero_stage(nc.gpsimd, 0, R, "w_st")
-        w2_st = zero_stage(nc.gpsimd, 64, R, "w2_st")
-        xo_s = zero_plane(nc.vector, T, "xo_s")
-        vs_s = zero_plane(nc.gpsimd, T, "vs_s")
-        load_plane(nc.gpsimd, vs_s, vs_scales)
-        l1 = load_list(offs, "l1")
-        xt_w = load_xt()
-        load_stage(nc.sync, xt_st, 0, xt_scales)
-        load_stage(nc.sync, w_st, 0, w_scales)
-        w_w = load_words(nc.sync, w_words, "w_w")
-        xo_w = load_words(nc.sync, xo_words, "xo_w")
-        l2 = load_list(offs2, "l2")
-        w2_w = load_words(nc.sync, w2_words, "w2_w")
-        load_plane(nc.sync, xo_s, xo_scales)
-        load_stage(nc.sync, w2_st, 64, w2_scales)
-        l4 = load_list(offs4, "l4")
-        l3 = load_list(offs3, "l3")
-        vs_w = load_words(nc.sync, vs_words, "vs_w")
-        l7 = load_list(offs7, "l7")
-        l6 = load_list(offs6, "l6")
-        l5 = load_list(offs5, "l5")
+        xt_stage = zero_stage(nc.vector, 0, TABLE, "xt_stage")
+        w_stage = zero_stage(nc.gpsimd, 0, R, "w_stage")
+        w2_stage = zero_stage(nc.gpsimd, HALF, R, "w2_stage")
+        xo_plane = zero_plane(nc.vector, "xo_plane")
+        vs_plane = zero_plane(nc.gpsimd, "vs_plane")
+        load_plane(nc.gpsimd, vs_plane, vs_scales)
+        list1 = load_list(offs, "list1")
+        xt_table = sb.tile([P, TABLE], U16, name="xt_table", align_bytes=64)
+        nc.sync.dma_start(xt_table[:].bitcast(I32), xt_words[0].bitcast(I32))
+        load_stage(xt_stage, 0, xt_scales)
+        load_stage(w_stage, 0, w_scales)
+        w_raw = load_words(w_words, "w_raw")
+        xo_table = load_words(xo_words, "xo_table")
+        list2 = load_list(offs2, "list2")
+        w2_raw = load_words(w2_words, "w2_raw")
+        load_stage(w2_stage, HALF, w2_scales)
+        load_plane(nc.sync, xo_plane, xo_scales)
+        list3 = load_list(offs3, "list3")
+        list4 = load_list(offs4, "list4")
+        vs_table = load_words(vs_words, "vs_table")
+        list7 = load_list(offs7, "list7")
+        list6 = load_list(offs6, "list6")
+        list5 = load_list(offs5, "list5")
 
-        xt_s = sb.tile([P, T], U8, name="xt_s", align_bytes=64)
-        move_half(xt_s, 0, xt_st, 0)
-        move_half(xt_s, 1, xt_st, 0)
-        move_half(w_st[:, 0, :], 1, w_st, 0)
-        xt_g = gather(xt_w, l1, "xt_g")
-        xts_g = gather(xt_s, l1, "xts_g")
-        ws_d = deal_bytes(w_st[:, 0, :], "ws_d")
-        w_d = deal(nc.scalar.copy, w_w, "w_d")
-        w2_d = deal(nc.scalar.copy, w2_w, "w2_d")
-        xo_g = gather(xo_w, l2, "xo_g")
-        move_half(w2_st[:, 1, :], 0, w2_st, 64)
-        w2s_d = deal_bytes(w2_st[:, 1, :], "w2s_d")
-        xos_g = gather(xo_s, l2, "xos_g")
+        xt_plane = sb.tile([P, TABLE], U8, name="xt_plane", align_bytes=64)
+        move_half(xt_plane, 0, xt_stage, 0)
+        move_half(xt_plane, 1, xt_stage, 0)
+        move_half(w_stage[:, 0, :], 1, w_stage, 0)
+        xt_picked = gather(xt_table, list1, "xt_picked")
+        xt_picked_scales = gather(xt_plane, list1, "xt_picked_scales")
+        w_dealt_scales = deal_bytes(w_stage[:, 0, :], "w_dealt_scales")
+        w_dealt = deal_words(w_raw, "w_dealt")
+        w2_dealt = deal_words(w2_raw, "w2_dealt")
 
-        a_sb, b_sb = [], []
+        early, late = slice(0, J // 2), slice(J // 2, J)
+        xo_picked = sb.tile([P, J], U32, name="xo_picked", align_bytes=64)
+        xo_picked_scales = sb.tile([P, J], U8, name="xo_picked_scales", align_bytes=64)
+        nc.vector.tensor_copy(xo_picked[:, early], xo_table[:].indirect(entries(list2, early)))
+        move_half(w2_stage[:, 1, :], 0, w2_stage, HALF)
+        w2_dealt_scales = deal_bytes(w2_stage[:, 1, :], "w2_dealt_scales")
+        nc.vector.tensor_copy(xo_picked_scales[:, early], xo_plane[:].indirect(entries(list2, early)))
+        nc.vector.tensor_copy(xo_picked[:, late], xo_table[:].indirect(entries(list2, late)))
+        nc.vector.tensor_copy(xo_picked_scales[:, late], xo_plane[:].indirect(entries(list2, late)))
+
+        a_rows, b_rows = [], []
         for t in range(PACK):
             cols = slice(t * P, (t + 1) * P)
             acc = ps.tile([P, J], F32, name="acc_a%d" % t, tag="bank%d" % t)
-            nc.tensor.matmul_mx(out=acc[:], lhsT=w_d[:, cols].bitcast(E5M2X4), lhsT_scale=ws_d[:, cols],
-                                rhs=xt_g[:].bitcast(E2M1X4), rhs_scale=xts_g[:], start=True, stop=True)
+            nc.tensor.matmul_mx(
+                out=acc[:], lhsT=w_dealt[:, cols].bitcast(E5M2X4), lhsT_scale=w_dealt_scales[:, cols],
+                rhs=xt_picked[:].bitcast(E2M1X4), rhs_scale=xt_picked_scales[:], start=True, stop=True,
+            )
             rows = sb.tile([P, WIDE], F32, name="a%d" % t)
             nc.scalar.copy(rows[:, :J], acc[:])
-            a_sb.append(rows)
+            a_rows.append(rows)
 
         for t in range(PACK):
             cols = slice(t * P, (t + 1) * P)
-            acc = ps.tile([P, J], F32, name="acc_b%d" % t, tag="bank%d" % (PACK + t))
-            nc.tensor.matmul_mx(out=acc[:], lhsT=w2_d[:, cols].bitcast(E4M3X4), lhsT_scale=w2s_d[:, cols],
-                                rhs=xo_g[:].bitcast(E5M2X4), rhs_scale=xos_g[:], start=True, stop=True)
             rows = sb.tile([P, WIDE], F32, name="b%d" % t)
-            nc.vector.tensor_copy(rows[:, :J], acc[:])
-            b_sb.append(rows)
+            for bank, slots in ((PACK, early), (0, late)) if t == 0 else ((PACK + t, slice(0, J)),):
+                acc = ps.tile([P, slots.stop - slots.start], F32, name="acc_b%d" % t, tag="bank%d" % bank)
+                nc.tensor.matmul_mx(
+                    out=acc[:], lhsT=w2_dealt[:, cols].bitcast(E4M3X4), lhsT_scale=w2_dealt_scales[:, cols],
+                    rhs=xo_picked[:, slots].bitcast(E5M2X4), rhs_scale=xo_picked_scales[:, slots],
+                    start=True, stop=True,
+                )
+                nc.vector.tensor_copy(rows[:, slots], acc[:])
+            b_rows.append(rows)
 
-        vs_g = gather(vs_w, l7, "vs_g")
-        vss_g = gather(vs_s, l7, "vss_g")
+        vs_picked = gather(vs_table, list7, "vs_picked")
 
         diff = sb.tile([P, PACK, O], F32, name="diff")
-
-        def place(t, parts):
-            second = sb.tile([P, O], F32, name="second%d" % t)
-            for cols, entries in parts:
-                if t >= 2:
-                    nc.scalar.activation(second[:, cols], h1[t][:].indirect(l6[:, entries]), ACT.Copy)
-                else:
-                    nc.vector.tensor_copy(second[:, cols], h1[t][:].indirect(l6[:, entries]))
-            for cols, entries in parts:
-                nc.vector.tensor_tensor(diff[:, t, cols], h1[t][:].indirect(l5[:, entries]), second[:, cols], ALU.subtract)
-
-        whole = [(slice(0, O), slice(0, O // 16))]
-        halves = [(slice(0, O // 2), slice(0, O // 32)), (slice(O // 2, O), slice(O // 32, O // 16))]
-        h1 = []
+        halves = [slice(0, O // 2), slice(O // 2, O)]
         for t in range(PACK):
-            pa = sb.tile([P, I], F32, name="pa%d" % t, tag="pa", bufs=2)
-            pb = sb.tile([P, I], F32, name="pb%d" % t, tag="pb", bufs=2)
-            nc.scalar.activation(pb[:], b_sb[t][:].indirect(l4[:]), ACT.Copy, scale=a_sb[t][:, 0:1])
-            nc.scalar.activation(pa[:], a_sb[t][:].indirect(l3[:]), ACT.Copy, scale=b_sb[t][:, 0:1])
-            kept = sb.tile([P, I], F32, name="h1_%d" % t)
-            nc.vector.tensor_tensor(kept[:], pa[:], pb[:], ALU.max)
-            h1.append(kept)
-            place(t, whole if t < PACK - 1 else halves)
+            a_picked = sb.tile([P, I], F32, name="a_picked%d" % t, tag="a_picked", bufs=2)
+            b_picked = sb.tile([P, I], F32, name="b_picked%d" % t, tag="b_picked", bufs=2)
+            nc.scalar.activation(a_picked[:], a_rows[t][:].indirect(list3[:]), ACT.Copy, scale=b_rows[t][:, 0:1])
+            nc.scalar.activation(b_picked[:], b_rows[t][:].indirect(list4[:]), ACT.Copy, scale=a_rows[t][:, 0:1])
+            h1 = sb.tile([P, I], F32, name="h1_%d" % t)
+            nc.vector.tensor_tensor(h1[:], a_picked[:], b_picked[:], ALU.max)
+
+            parts = halves if t == PACK - 1 else [slice(0, O)]
+            second = sb.tile([P, O], F32, name="second%d" % t, align_bytes=64)
+            for places in parts:
+                looked_up = h1[:].indirect(entries(list6, places))
+                if t >= PACK - 2:
+                    nc.scalar.activation(second[:, places], looked_up, ACT.Copy)
+                else:
+                    nc.vector.tensor_copy(second[:, places], looked_up)
+            for places in parts:
+                nc.vector.tensor_tensor(
+                    diff[:, t, places], h1[:].indirect(entries(list5, places)), second[:, places], ALU.subtract
+                )
+
+        vs_picked_scales = sb.tile([P, N], U8, name="vs_picked_scales", tag="second%d" % (PACK - 1), align_bytes=64)
+        nc.vector.tensor_copy(vs_picked_scales[:], vs_plane[:].indirect(list7[:]))
 
         hid = sb.tile([P, O, PACK], BF16, name="hid", align_bytes=64)
         woven = diff[:].rearrange("p t o -> p o t")
-        hid_w = sb.tile([P, O], U32, name="hid_w", align_bytes=64)
-        hid_s = sb.tile([P, O], U8, name="hid_s", align_bytes=64)
-        for cols, entries in halves:
-            nc.scalar.activation(hid[:, cols, :], woven[:, cols, :], ACT.Abs)
-            nc.vector.quantize_mx(out=hid_w[:, cols].bitcast(E5M2X4), scales=hid_s[:, cols], in_=hid[:, cols, :].rearrange("p o t -> p (o t)"))
+        hid_words = sb.tile([P, O], U32, name="hid_words", align_bytes=64)
+        hid_scales = sb.tile([P, O], U8, name="hid_scales", align_bytes=64)
+        for places in halves:
+            nc.scalar.activation(hid[:, places, :], woven[:, places, :], ACT.Abs)
+            nc.vector.quantize_mx(
+                out=hid_words[:, places].bitcast(E5M2X4), scales=hid_scales[:, places],
+                in_=hid[:, places, :].rearrange("p o t -> p (o t)"),
+            )
 
         for h, (copy, queue) in enumerate(((nc.vector.tensor_copy, nc.sync), (nc.scalar.copy, nc.scalar))):
             cols = slice(h * P, (h + 1) * P)
             acc = ps.tile([P, O], F32, name="acc_y%d" % h, tag="bank%d" % h)
-            nc.tensor.matmul_mx(out=acc[:], lhsT=vs_g[:, cols].bitcast(E4M3X4), lhsT_scale=vss_g[:, cols],
-                                rhs=hid_w[:].bitcast(E5M2X4), rhs_scale=hid_s[:], start=True, stop=True)
+            nc.tensor.matmul_mx(
+                out=acc[:], lhsT=vs_picked[:, cols].bitcast(E4M3X4), lhsT_scale=vs_picked_scales[:, cols],
+                rhs=hid_words[:].bitcast(E5M2X4), rhs_scale=hid_scales[:], start=True, stop=True,
+            )
             y = sb.tile([P, O], F32, name="y%d" % h)
             copy(y[:], acc[:])
             queue.dma_start(out[cols, :], y[:])

from contextlib import ExitStack

import concourse.mybir as mybir

F32 = mybir.dt.float32
BF16 = mybir.dt.bfloat16
I32 = mybir.dt.int32
U32 = mybir.dt.uint32
U16 = mybir.dt.uint16
U8 = mybir.dt.uint8
E2M1X4 = mybir.dt.float4_e2m1fn_x4
E5M2X4 = mybir.dt.float8_e5m2_x4
E4M3X4 = mybir.dt.float8_e4m3fn_x4
ALU = mybir.AluOpType
ACT = mybir.ActivationFunctionType

P = 128
PACK = 4
QUADRANT = 32
HALF = 64
PER_COLUMN = 16
TABLE = 1024
J, R, I, O, N = 256, 512, 256, 128, 256
WIDE = 2 * J
FLOPS = 2 * 512 * R * J * 2 + 2 * R * N * O


def tile_list_leadmeetthenlook_twotab_store_plain_kernel(
    tc, xt_words, xt_scales, xo_words, xo_scales, w_words, w_scales, w2_words, w2_scales, vs_words, vs_scales,
    offs, offs2, offs3, offs4, offs5, offs6, offs7, out,
):
    nc = tc.nc
    with ExitStack() as ctx:
        sb = ctx.enter_context(tc.tile_pool(name="sb", bufs=1))
        ps = ctx.enter_context(tc.psum_pool(name="ps", bufs=1))

        def load_list(src, name):
            tile = sb.tile(list(src.shape), U16, name=name)
            nc.sync.dma_start(tile[:], src)
            return tile

        def load_words(src, name):
            tile = sb.tile([P, src.shape[2]], U32, name=name, align_bytes=64)
            nc.sync.dma_start(tile[:].bitcast(I32), src[0].rearrange("p c t -> p (c t)").bitcast(I32))
            return tile

        def zero_plane(engine, name):
            tile = sb.tile([P, TABLE], U8, name=name, align_bytes=64)
            engine.memset(tile[:].bitcast(I32), 0)
            return tile

        def load_plane(queue, plane, src):
            for r in range(PACK):
                queue.dma_start(plane[r:P:QUADRANT, :].bitcast(I32), src[0, r:16:PACK, :].bitcast(I32))

        def zero_stage(engine, base, width, name):
            tile = sb.tile([P, 2, width], U8, name=name, align_bytes=64)
            engine.memset(tile[base : base + HALF].rearrange("p h c -> p (h c)").bitcast(I32), 0)
            return tile

        def load_stage(stage, base, src):
            rows = src[0].bitcast(I32).rearrange("(h q r) c -> q r h c", h=2, q=2)
            for q in range(2):
                first = base + QUADRANT * q
                nc.sync.dma_start(stage[first : first + PACK].bitcast(I32), rows[q])

        def move_half(plane, h, stage, base):
            nc.vector.tensor_copy(
                plane[HALF * h : HALF * (h + 1)].bitcast(I32), stage[base : base + HALF, h, :].bitcast(I32)
            )

        def entries(offsets, picks):
            return offsets[:, picks.start // PER_COLUMN : picks.stop // PER_COLUMN]

        def gather(window, offsets, name):
            tile = sb.tile([P, PER_COLUMN * offsets.shape[1]], window.dtype, name=name, align_bytes=64)
            nc.vector.tensor_copy(tile[:], window[:].indirect(offsets[:]))
            return tile

        def deal_words(src, name):
            tile = sb.tile([P, R], U32, name=name, align_bytes=64)
            nc.scalar.copy(
                tile[:].rearrange("p (t c i) -> p c t i", t=PACK, i=4),
                src[:].rearrange("p (c i t) -> p c t i", t=PACK, i=4),
            )
            return tile

        def deal_bytes(plane, name):
            tile = sb.tile([P, R], U8, name=name, align_bytes=64)
            nc.vector.tensor_copy(
                tile[:].rearrange("p (t m) -> p t m", t=PACK), plane.rearrange("p (m t) -> p t m", t=PACK)
            )
            return tile

        xt_stage = zero_stage(nc.vector, 0, TABLE, "xt_stage")
        w_stage = zero_stage(nc.gpsimd, 0, R, "w_stage")
        w2_stage = zero_stage(nc.gpsimd, HALF, R, "w2_stage")
        xo_plane = zero_plane(nc.vector, "xo_plane")
        vs_plane = zero_plane(nc.gpsimd, "vs_plane")
        load_plane(nc.gpsimd, vs_plane, vs_scales)
        list1 = load_list(offs, "list1")
        xt_table = sb.tile([P, TABLE], U16, name="xt_table", align_bytes=64)
        nc.sync.dma_start(xt_table[:].bitcast(I32), xt_words[0].bitcast(I32))
        load_stage(xt_stage, 0, xt_scales)
        load_stage(w_stage, 0, w_scales)
        w_raw = load_words(w_words, "w_raw")
        xo_table = load_words(xo_words, "xo_table")
        list2 = load_list(offs2, "list2")
        w2_raw = load_words(w2_words, "w2_raw")
        load_stage(w2_stage, HALF, w2_scales)
        load_plane(nc.sync, xo_plane, xo_scales)
        list3 = load_list(offs3, "list3")
        list4 = load_list(offs4, "list4")
        vs_table = load_words(vs_words, "vs_table")
        list7 = load_list(offs7, "list7")
        list6 = load_list(offs6, "list6")
        list5 = load_list(offs5, "list5")

        xt_plane = sb.tile([P, TABLE], U8, name="xt_plane", align_bytes=64)
        move_half(xt_plane, 0, xt_stage, 0)
        move_half(xt_plane, 1, xt_stage, 0)
        move_half(w_stage[:, 0, :], 1, w_stage, 0)
        xt_picked = gather(xt_table, list1, "xt_picked")
        xt_picked_scales = gather(xt_plane, list1, "xt_picked_scales")
        w_dealt_scales = deal_bytes(w_stage[:, 0, :], "w_dealt_scales")
        w_dealt = deal_words(w_raw, "w_dealt")
        w2_dealt = deal_words(w2_raw, "w2_dealt")

        early, late = slice(0, J // 2), slice(J // 2, J)
        xo_picked = sb.tile([P, J], U32, name="xo_picked", align_bytes=64)
        xo_picked_scales = sb.tile([P, J], U8, name="xo_picked_scales", align_bytes=64)
        nc.vector.tensor_copy(xo_picked[:, early], xo_table[:].indirect(entries(list2, early)))
        move_half(w2_stage[:, 1, :], 0, w2_stage, HALF)
        w2_dealt_scales = deal_bytes(w2_stage[:, 1, :], "w2_dealt_scales")
        nc.vector.tensor_copy(xo_picked_scales[:, early], xo_plane[:].indirect(entries(list2, early)))
        nc.vector.tensor_copy(xo_picked[:, late], xo_table[:].indirect(entries(list2, late)))
        nc.vector.tensor_copy(xo_picked_scales[:, late], xo_plane[:].indirect(entries(list2, late)))

        a_rows, b_rows = [], []
        for t in range(PACK):
            cols = slice(t * P, (t + 1) * P)
            acc = ps.tile([P, J], F32, name="acc_a%d" % t, tag="bank%d" % t)
            nc.tensor.matmul_mx(
                out=acc[:], lhsT=w_dealt[:, cols].bitcast(E5M2X4), lhsT_scale=w_dealt_scales[:, cols],
                rhs=xt_picked[:].bitcast(E2M1X4), rhs_scale=xt_picked_scales[:], start=True, stop=True,
            )
            rows = sb.tile([P, WIDE], F32, name="a%d" % t)
            nc.scalar.copy(rows[:, :J], acc[:])
            a_rows.append(rows)

        for t in range(PACK):
            cols = slice(t * P, (t + 1) * P)
            rows = sb.tile([P, WIDE], F32, name="b%d" % t)
            for bank, slots in ((PACK, early), (0, late)) if t == 0 else ((PACK + t, slice(0, J)),):
                acc = ps.tile([P, slots.stop - slots.start], F32, name="acc_b%d" % t, tag="bank%d" % bank)
                nc.tensor.matmul_mx(
                    out=acc[:], lhsT=w2_dealt[:, cols].bitcast(E4M3X4), lhsT_scale=w2_dealt_scales[:, cols],
                    rhs=xo_picked[:, slots].bitcast(E5M2X4), rhs_scale=xo_picked_scales[:, slots],
                    start=True, stop=True,
                )
                nc.vector.tensor_copy(rows[:, slots], acc[:])
            b_rows.append(rows)

        vs_picked = gather(vs_table, list7, "vs_picked")

        diff = sb.tile([P, PACK, O], F32, name="diff")
        halves = [slice(0, O // 2), slice(O // 2, O)]
        for t in range(PACK):
            a_picked = sb.tile([P, I], F32, name="a_picked%d" % t, tag="a_picked", bufs=2)
            b_picked = sb.tile([P, I], F32, name="b_picked%d" % t, tag="b_picked", bufs=2)
            nc.scalar.activation(a_picked[:], a_rows[t][:].indirect(list3[:]), ACT.Copy, scale=b_rows[t][:, 0:1])
            nc.scalar.activation(b_picked[:], b_rows[t][:].indirect(list4[:]), ACT.Copy, scale=a_rows[t][:, 0:1])
            h1 = sb.tile([P, I], F32, name="h1_%d" % t)
            nc.vector.tensor_tensor(h1[:], a_picked[:], b_picked[:], ALU.max)

            parts = halves if t == PACK - 1 else [slice(0, O)]
            second = sb.tile([P, O], F32, name="second%d" % t, align_bytes=64)
            for places in parts:
                looked_up = h1[:].indirect(entries(list6, places))
                if t >= PACK - 2:
                    nc.scalar.activation(second[:, places], looked_up, ACT.Copy)
                else:
                    nc.vector.tensor_copy(second[:, places], looked_up)
            for places in parts:
                nc.vector.tensor_tensor(
                    diff[:, t, places], h1[:].indirect(entries(list5, places)), second[:, places], ALU.subtract
                )

        vs_picked_scales = sb.tile([P, N], U8, name="vs_picked_scales", tag="second%d" % (PACK - 1), align_bytes=64)
        nc.vector.tensor_copy(vs_picked_scales[:], vs_plane[:].indirect(list7[:]))

        hid = sb.tile([P, O, PACK], BF16, name="hid", align_bytes=64)
        woven = diff[:].rearrange("p t o -> p o t")
        hid_words = sb.tile([P, O], U32, name="hid_words", align_bytes=64)
        hid_scales = sb.tile([P, O], U8, name="hid_scales", align_bytes=64)
        for places in halves:
            nc.scalar.activation(hid[:, places, :], woven[:, places, :], ACT.Abs)
            nc.vector.quantize_mx(
                out=hid_words[:, places].bitcast(E5M2X4), scales=hid_scales[:, places],
                in_=hid[:, places, :].rearrange("p o t -> p (o t)"),
            )

        for h, (copy, queue) in enumerate(((nc.vector.tensor_copy, nc.sync), (nc.scalar.copy, nc.scalar))):
            cols = slice(h * P, (h + 1) * P)
            acc = ps.tile([P, O], F32, name="acc_y%d" % h, tag="bank%d" % h)
            nc.tensor.matmul_mx(
                out=acc[:], lhsT=vs_picked[:, cols].bitcast(E4M3X4), lhsT_scale=vs_picked_scales[:, cols],
                rhs=hid_words[:].bitcast(E5M2X4), rhs_scale=hid_scales[:], start=True, stop=True,
            )
            y = sb.tile([P, O], F32, name="y%d" % h)
            copy(y[:], acc[:])
            queue.dma_start(out[cols, :], y[:])
